import numpy as np
import ml_dtypes


def mxq(x, axis, fmt="e4m3"):
    dtype, down = {"e4m3": (ml_dtypes.float8_e4m3fn, 7), "e5m2": (ml_dtypes.float8_e5m2, 14)}[fmt]
    v = np.moveaxis(np.asarray(x, np.float32).astype(ml_dtypes.bfloat16).astype(np.float64), axis, -1)
    blocks = v.reshape(v.shape[:-1] + (-1, 32))
    amax = np.abs(blocks).max(-1, keepdims=True)
    byte = np.maximum(np.where(amax > 0, np.frexp(amax)[1] - 1 + 127, 0) - down, 1)
    scale = np.exp2(byte - 127.0)
    codes = (blocks / scale).astype(np.float32).astype(dtype).astype(np.float64)
    return np.moveaxis((codes * scale).reshape(v.shape), -1, axis)


WIDE = False


def mx_kscale(k):
    if not WIDE:
        return np.ones(k)
    levels = np.array([10, -10, 5, -5, 0])
    if k % 512:
        return np.exp2(np.random.permutation(np.resize(levels, k // 32))).repeat(32)
    a = np.empty((k // 512, 16))
    for p in range(k // 512):
        a[p, :8] = np.random.permutation(np.resize(levels, 8))
        for g in range(8):
            far = levels[np.abs(levels - a[p, g]) >= 10]
            a[p, g + 8] = far[np.random.randint(len(far))]
    return np.exp2(a.ravel()).repeat(32)


def f64(x):
    return np.asarray(x).astype(np.float64)


def striped(idx):
    return np.tile(idx.reshape(-1, 16).T, (8, 1)).astype(np.uint16)


def unstriped(offs):
    return offs[:16].T.reshape(-1).astype(np.int64)


E2M1 = np.array([0.0, 0.5, 1.0, 1.5, 2.0, 3.0, 4.0, 6.0, -0.0, -0.5, -1.0, -1.5, -2.0, -3.0, -4.0, -6.0])


def pack_weight(w, fmt):
    k, n = w.shape
    w = f64(np.asarray(w, np.float32).astype(ml_dtypes.bfloat16)).reshape(k // 32, 32, n)
    amax = np.abs(w).max(1)
    if fmt == "e4m3":
        byte = np.frexp(amax)[1] - 1 + 127 - 7
    else:
        mant, ex = np.frexp(amax / 6.0)
        byte = np.where(mant > 0.5, ex, ex - 1) + 127
    byte = np.clip(np.where(amax > 0, byte, 1), 1, 254)
    scaled = (w * np.exp2(127.0 - byte)[:, None, :]).reshape(k, n).astype(np.float32)
    by_word = np.ascontiguousarray(scaled.reshape(k // 512, 128, 4, n).transpose(0, 1, 3, 2))
    if fmt == "e4m3":
        words = by_word.astype(ml_dtypes.float8_e4m3fn).view(np.uint8)
    else:
        c = by_word.astype(ml_dtypes.float4_e2m1fn).view(np.uint8) & 0xF
        words = (c[..., 0::2] | (c[..., 1::2] << 4)).reshape(k // 512, 128, 2 * n)
    return np.ascontiguousarray(words), np.ascontiguousarray(byte.astype(np.uint8).reshape(k // 512, 16, n))


def unpack_weight(words, scales, fmt):
    g, _, n = scales.shape
    words = np.ascontiguousarray(words).reshape(g, 128, n, -1)
    if fmt == "e4m3":
        vals = words.view(ml_dtypes.float8_e4m3fn).astype(np.float64)
    else:
        nib = np.empty((g, 128, n, 4), np.uint8)
        nib[..., 0::2] = words & 0xF
        nib[..., 1::2] = words >> 4
        vals = E2M1[nib]
    vals = vals * np.repeat(np.exp2(scales.astype(np.float64) - 127.0), 8, axis=1)[..., None]
    return vals.transpose(0, 1, 3, 2).reshape(g * 512, n)


def gelu(v):
    return 0.5 * v * (1.0 + np.tanh(np.sqrt(2.0 / np.pi) * (v + 0.044715 * v**3)))


def twice(P):
    return np.random.permutation(np.repeat(np.arange(P), 2))


K, T, S, P, H = 1536, 4096, 1024, 512, 512

def setup_inputs():
    n = np.random.standard_normal
    s = mx_kscale(K)[:, None]
    u = mx_kscale(H)[:, None]
    d = {}
    d["tab_words"], d["tab_scales"] = pack_weight(n((K, T)) * s, "e4m3")
    d["offs"] = striped(np.random.permutation(T)[:S])
    d["pos1"] = striped(np.random.permutation(S)[:P])
    d["pos2"] = striped(np.random.permutation(S)[:P])
    d["pos3"] = striped(twice(P))
    d["w1"] = (0.56 * n((K, H)) / K ** 0.5 / s).astype(np.float32)
    d["w4_words"], d["w4_scales"] = pack_weight(0.56 * n((K, H)) / K ** 0.5 / s, "e2m1")
    d["gain"] = (np.random.uniform(0.7, 1.3, H) * u[:, 0]).astype(np.float32)
    d["w2"] = (n((H, H)) / H ** 0.5 / u).astype(np.float32)
    d["rg"] = (np.random.uniform(0.8, 1.1, H) / u[:, 0]).astype(np.float32)
    return d

def reference(tab_words, tab_scales, offs, pos1, pos2, pos3, w1, w4_words, w4_scales, gain, w2, rg):
    v = unpack_weight(tab_words, tab_scales, "e4m3")[:, unstriped(offs)]
    swing = mxq(f64(w1), 0, "e4m3").T @ v
    drift = unpack_weight(w4_words, w4_scales, "e2m1").T @ v
    h = f64(gain)[:, None] * (np.sin(swing) + np.cos(drift))
    x = np.maximum(h[:, unstriped(pos1)], h[:, unstriped(pos2)])
    y = mxq(f64(w2), 0, "e4m3").T @ mxq(x, 0, "e4m3")
    hs = f64(rg)[:, None] * h
    return y[:, unstriped(pos3)] * np.cos(hs) - hs

@@ -1,0 +1,290 @@
+import math
+from contextlib import ExitStack
+
+import concourse.mybir as mybir
+
+K, T, S, M, H = 1536, 4096, 1024, 512, 512
+FLOPS = 2 * K * H * S * 2 + 2 * H * H * M
+
+F32 = mybir.dt.float32
+BF16 = mybir.dt.bfloat16
+I32 = mybir.dt.int32
+U32 = mybir.dt.uint32
+U16 = mybir.dt.uint16
+U8 = mybir.dt.uint8
+FP8X4 = mybir.dt.float8_e4m3fn_x4
+FP4X4 = mybir.dt.float4_e2m1fn_x4
+ACT = mybir.ActivationFunctionType
+ALU = mybir.AluOpType
+
+P = 128
+PACK = 4
+PASSES = K // (P * PACK)
+BANK = 512
+HALVES = S // BANK
+SPARE = 16
+SHIFT_ROWS = 112
+
+
+def tile_list_rifle_sway_evaluator_kernel(
+    tc, tab_words, tab_scales, offs, pos1, pos2, pos3, w1, w4_words, w4_scales, gain, w2, rg, out
+):
+    nc = tc.nc
+    with ExitStack() as ctx:
+        keep = ctx.enter_context(tc.tile_pool(name="keep", bufs=1))
+        ring = ctx.enter_context(tc.tile_pool(name="ring", bufs=2))
+        psum = ctx.enter_context(tc.psum_pool(name="psum", bufs=1))
+
+        def held(shape, dtype, name):
+            return keep.tile(shape, dtype, name=name, align_bytes=64)
+
+        idx = keep.tile([P, S // 16], U16, name="idx")
+        p1 = keep.tile([P, M // 16], U16, name="p1")
+        p2 = keep.tile([P, M // 16], U16, name="p2")
+        p3 = keep.tile([P, S // 16], U16, name="p3")
+
+        table_scales = held([P, T], U8, "table_scales")
+        w4_scales_raw = held([P, PASSES, H], U8, "w4_scales_raw")
+        v_scales = [held([P, S], U8, f"v_scales{a}") for a in range(PASSES)]
+        nc.vector.memset(table_scales[:].bitcast(I32), 0)
+        nc.vector.memset(w4_scales_raw[:].rearrange("p a c -> p (a c)").bitcast(I32), 0)
+        for a in range(1, PASSES):
+            nc.vector.memset(v_scales[a][:].bitcast(I32), 0)
+
+        nc.sync.dma_start(idx[:], offs)
+        gain_sb = held([P, PACK], F32, "gain_sb")
+        nc.sync.dma_start(gain_sb[:], gain.rearrange("(p t) -> p t", t=PACK))
+        w4_raw = held([P, PASSES, 2 * H], U8, "w4_raw")
+        nc.sync.dma_start(w4_raw[:].bitcast(I32), w4_words.rearrange("a p c -> p a c").bitcast(I32))
+        table = [held([P, T], I32, f"table{a}") for a in range(PASSES)]
+        for a in range(PASSES):
+            nc.sync.dma_start(table[a][:], tab_words[a].rearrange("p t i -> p (t i)").bitcast(I32))
+        w1_rows = w1.rearrange("(a p i) c -> a p i c", p=P, i=PACK)
+        w1_raw = []
+        for a in range(PASSES):
+            parts = 2 if a == PASSES - 1 else 1
+            width = H // parts
+            w1_raw.append([held([P, PACK, width], F32, f"w1_raw{a}_{u}") for u in range(parts)])
+            for u in range(parts):
+                nc.sync.dma_start(w1_raw[a][u][:], w1_rows[a][:, :, u * width : (u + 1) * width])
+        rg_sb = held([P, PACK], F32, "rg_sb")
+        nc.sync.dma_start(p1[:], pos1)
+        nc.sync.dma_start(p2[:], pos2)
+        nc.sync.dma_start(rg_sb[:], rg.rearrange("(p t) -> p t", t=PACK))
+        nc.sync.dma_start(p3[:], pos3)
+        w2_raw = held([P, PACK, H], F32, "w2_raw")
+        nc.sync.dma_start(w2_raw[:], w2.rearrange("(p i) c -> p i c", i=PACK))
+
+        for q in range(4):
+            nc.gpsimd.dma_start(
+                table_scales[32 * q : 32 * q + 4 * PASSES, :].bitcast(I32),
+                tab_scales[:, 4 * q : 4 * q + 4, :].bitcast(I32),
+            )
+        for q in range(4):
+            nc.gpsimd.dma_start(
+                w4_scales_raw[32 * q : 32 * q + 4, :, :].bitcast(I32),
+                w4_scales[:, 4 * q : 4 * q + 4, :].rearrange("a r c -> r a c").bitcast(I32),
+            )
+
+        nc.vector.tensor_copy(v_scales[0][:], table_scales[:].indirect(idx[:]))
+        for a in range(1, PASSES):
+            nc.gpsimd.dma_start(
+                v_scales[a][0:SHIFT_ROWS, :].bitcast(I32),
+                v_scales[0][4 * a : 4 * a + SHIFT_ROWS, :].bitcast(I32),
+            )
+
+        w4_codes = held([P, PASSES, 2 * H], U8, "w4_codes")
+        w4_planes = held([P, PASSES, H], U8, "w4_planes")
+        nc.vector.tensor_copy(
+            w4_codes[:].bitcast(U16).rearrange("p a (t m) -> p a m t", t=PACK),
+            w4_raw[:].bitcast(U16).rearrange("p a (m t) -> p a m t", t=PACK),
+        )
+        nc.vector.tensor_copy(
+            w4_planes[:].rearrange("p a (t m) -> p a m t", t=PACK),
+            w4_scales_raw[:].rearrange("p a (m t) -> p a m t", t=PACK),
+        )
+
+        gain_wide = [held([P, M], F32, f"gain_wide{t}") for t in range(PACK)]
+        for t in range(PACK):
+            nc.vector.tensor_copy(gain_wide[t][:], gain_sb[:, t : t + 1].to_broadcast([P, M]))
+
+        v_codes = [held([P, S], U32, f"v_codes{a}") for a in range(PASSES)]
+        for a in range(PASSES):
+            window = table[a][:].bitcast(U32)
+            if a < PASSES - 1:
+                nc.vector.tensor_copy(v_codes[a][:], window.indirect(idx[:]))
+            else:
+                for u in range(HALVES):
+                    nc.vector.tensor_copy(
+                        v_codes[a][:, u * BANK : (u + 1) * BANK],
+                        window.indirect(idx[:, u * BANK // 16 : (u + 1) * BANK // 16]),
+                    )
+
+        def bank(b):
+            return psum.tile([P, BANK], F32, name=f"bank{b}")
+
+        def cols(u):
+            return slice(u * BANK, (u + 1) * BANK)
+
+        def rows(t):
+            return slice(t * P, (t + 1) * P)
+
+        drift = [[bank(HALVES * t + u) for u in range(HALVES)] for t in range(PACK)]
+        for a in range(PASSES):
+            for u in range(HALVES):
+                for t in range(PACK):
+                    nc.tensor.matmul_mx(
+                        drift[t][u][:],
+                        lhsT=w4_codes[:, a, 2 * t * P : 2 * (t + 1) * P].bitcast(FP4X4),
+                        lhsT_scale=w4_planes[:, a, rows(t)],
+                        rhs=v_codes[a][:, cols(u)].bitcast(FP8X4),
+                        rhs_scale=v_scales[a][:, cols(u)],
+                        start=(a == 0),
+                        stop=(a == PASSES - 1),
+                    )
+        cos_part = [held([P, S], F32, f"cos_part{t}") for t in range(PACK)]
+
+        def drift_out(t):
+            for u in range(HALVES):
+                nc.scalar.activation(cos_part[t][:, cols(u)], drift[t][u][:], ACT.Sin, scale=0.5)
+
+        def drift_square(t):
+            nc.scalar.activation(cos_part[t][:], cos_part[t][:], ACT.Square, scale=math.sqrt(2.0))
+
+        drift_out(0)
+        drift_out(1)
+        drift_square(0)
+        drift_out(2)
+        drift_out(3)
+
+        def deal(dst, src, m0, m1):
+            return (
+                dst[:].rearrange("p (t m i) -> p m t i", t=PACK, i=PACK)[:, m0:m1],
+                src[:].rearrange("p i (m t) -> p m t i", t=PACK),
+            )
+
+        w1_codes = [held([P, H], U32, f"w1_codes{a}") for a in range(PASSES)]
+        w1_planes = [held([P, H], U8, f"w1_planes{a}") for a in range(PASSES)]
+        for a in range(PASSES):
+            rounded = ring.tile([P, PACK * H], BF16, name="rounded", align_bytes=64)
+            parts = len(w1_raw[a])
+            for u in range(parts):
+                nc.vector.tensor_copy(*deal(rounded, w1_raw[a][u], u * P // parts, (u + 1) * P // parts))
+            if a < PASSES - 1:
+                nc.vector.quantize_mx(w1_codes[a][:].bitcast(FP8X4), w1_planes[a][:], rounded[:])
+            else:
+                for t in range(PACK):
+                    nc.vector.quantize_mx(
+                        w1_codes[a][:, rows(t)].bitcast(FP8X4),
+                        w1_planes[a][:, rows(t)],
+                        rounded[:, t * H : (t + 1) * H],
+                    )
+
+        rg_neg = held([P, PACK], F32, "rg_neg")
+        nc.vector.scalar_tensor_tensor(rg_neg[:], rg_sb[:], -1.0, gain_sb[:], ALU.mult, ALU.mult)
+
+        swing = [[bank(HALVES * t + u) for u in range(HALVES)] for t in range(PACK)]
+
+        def swing_pass(a, t):
+            for u in range(HALVES):
+                nc.tensor.matmul_mx(
+                    swing[t][u][:],
+                    lhsT=w1_codes[a][:, rows(t)].bitcast(FP8X4),
+                    lhsT_scale=w1_planes[a][:, rows(t)],
+                    rhs=v_codes[a][:, cols(u)].bitcast(FP8X4),
+                    rhs_scale=v_scales[a][:, cols(u)],
+                    start=(a == 0),
+                    stop=(a == PASSES - 1),
+                )
+
+        for t in range(PACK):
+            for a in range(PASSES):
+                swing_pass(a, t)
+
+        h = [held([P, S], F32, f"h{t}") for t in range(PACK)]
+        first = held([P, PACK, M], F32, "first")
+        second = held([P, PACK, M], F32, "second")
+
+        def make_h(t):
+            c = cos_part[t]
+            if t > 0:
+                drift_square(t)
+            sin_part = ring.tile([P, S], F32, name="sin_part")
+            for u in range(HALVES):
+                nc.scalar.activation(sin_part[:, cols(u)], swing[t][u][:], ACT.Sin)
+            spans = [cols(u) for u in range(HALVES)] if t == 0 else [slice(0, S)]
+            for span in spans:
+                nc.vector.scalar_tensor_tensor(
+                    h[t][:, span], sin_part[:, span], 1.0, c[:, span], ALU.add, ALU.subtract
+                )
+
+        make_h(0)
+        for t in range(PACK):
+            nc.vector.tensor_tensor(first[:, t, :], h[t][:].indirect(p1[:]), gain_wide[t][:], ALU.mult)
+            if t + 1 < PACK:
+                make_h(t + 1)
+            nc.vector.tensor_tensor(second[:, t, :], h[t][:].indirect(p2[:]), gain_wide[t][:], ALU.mult)
+
+        w2_rounded = ring.tile([P, PACK * H], BF16, name="rounded", align_bytes=64)
+        nc.scalar.copy(*deal(w2_rounded, w2_raw, 0, P))
+        w2_codes = held([P, H], U32, "w2_codes")
+        w2_plane = held([P, H], U8, "w2_plane")
+        nc.vector.quantize_mx(w2_codes[:].bitcast(FP8X4), w2_plane[:], w2_rounded[:])
+
+        cos_hs = [keep.tile([P, S], F32, name=f"cos_part{t}", align_bytes=64) for t in range(PACK)]
+
+        def make_cos_hs(t):
+            nc.scalar.activation(cos_hs[t][:], h[t][:], ACT.Abs, scale=rg_neg[:, t : t + 1])
+            nc.scalar.activation(cos_hs[t][:], cos_hs[t][:], ACT.Sin, scale=-1.0, bias=math.pi / 2)
+
+        make_cos_hs(0)
+
+        half = M // 2
+        x_rounded = [held([P, PACK * half], BF16, f"x_rounded{u}") for u in range(2)]
+        x_codes = [held([P, half], U32, f"x_codes{u}") for u in range(2)]
+        x_plane = [held([P, half], U8, f"x_plane{u}") for u in range(2)]
+        for u in range(2):
+            span = slice(u * half, (u + 1) * half)
+            nc.vector.tensor_tensor(
+                x_rounded[u][:].rearrange("p (c i t) -> p c t i", i=4, t=PACK),
+                first[:, :, span].rearrange("p t (c i) -> p c t i", i=4),
+                second[:, :, span].rearrange("p t (c i) -> p c t i", i=4),
+                ALU.max,
+            )
+        for u in range(2):
+            nc.vector.quantize_mx(x_codes[u][:].bitcast(FP8X4), x_plane[u][:], x_rounded[u][:])
+
+        y = [held([P, M + SPARE], F32, f"y{t}") for t in range(PACK)]
+        for t in range(PACK):
+            nc.gpsimd.memset(y[t][:, M:], 0.0)
+        for t in range(PACK):
+            for u in range(2):
+                acc = psum.tile([P, half], F32, name=f"bank{2 * t + u}")
+                nc.tensor.matmul_mx(
+                    acc[:],
+                    lhsT=w2_codes[:, rows(t)].bitcast(FP8X4),
+                    lhsT_scale=w2_plane[:, rows(t)],
+                    rhs=x_codes[u][:].bitcast(FP8X4),
+                    rhs_scale=x_plane[u][:],
+                    start=True,
+                    stop=True,
+                )
+                nc.scalar.copy(y[t][:, u * half : (u + 1) * half], acc[:])
+            if t + 1 < PACK:
+                make_cos_hs(t + 1)
+
+        out_rows = out.rearrange("(p t) j -> p t j", t=PACK)
+        for t in range(PACK):
+            scores = [held([P, BANK], F32, f"score{t}_{u}") for u in range(HALVES)]
+            for u in range(HALVES):
+                nc.vector.tensor_tensor(
+                    scores[u][:],
+                    y[t][:].indirect(p3[:, u * BANK // 16 : (u + 1) * BANK // 16]),
+                    cos_hs[t][:, cols(u)],
+                    ALU.mult,
+                )
+            for u in range(HALVES):
+                nc.vector.scalar_tensor_tensor(
+                    scores[u][:], h[t][:, cols(u)], rg_neg[:, t : t + 1], scores[u][:], ALU.mult, ALU.add
+                )
+                nc.sync.dma_start(out_rows[:, t, cols(u)], scores[u][:])

@@ -23,7 +23,7 @@ PASSES = K // (P * PACK)
 BANK = 512
 HALVES = S // BANK
 SPARE = 16
-SHIFT_ROWS = 112
+SHIFT_ROWS = 100
 
 
 def tile_list_rifle_sway_evaluator_kernel(
@@ -43,70 +43,73 @@ def tile_list_rifle_sway_evaluator_kernel(
         p2 = keep.tile([P, M // 16], U16, name="p2")
         p3 = keep.tile([P, S // 16], U16, name="p3")
 
-        table_scales = held([P, T], U8, "table_scales")
+        table_scales = held([P, T], U8, "region2")
         w4_scales_raw = held([P, PASSES, H], U8, "w4_scales_raw")
         v_scales = [held([P, S], U8, f"v_scales{a}") for a in range(PASSES)]
-        nc.vector.memset(table_scales[:].bitcast(I32), 0)
-        nc.vector.memset(w4_scales_raw[:].rearrange("p a c -> p (a c)").bitcast(I32), 0)
-        for a in range(1, PASSES):
-            nc.vector.memset(v_scales[a][:].bitcast(I32), 0)
-
-        nc.sync.dma_start(idx[:], offs)
+        w4_planes = held([P, PASSES, H], U8, "w4_planes")
         gain_sb = held([P, PACK], F32, "gain_sb")
-        nc.sync.dma_start(gain_sb[:], gain.rearrange("(p t) -> p t", t=PACK))
-        w4_raw = held([P, PASSES, 2 * H], U8, "w4_raw")
-        nc.sync.dma_start(w4_raw[:].bitcast(I32), w4_words.rearrange("a p c -> p a c").bitcast(I32))
-        table = [held([P, T], I32, f"table{a}") for a in range(PASSES)]
-        for a in range(PASSES):
-            nc.sync.dma_start(table[a][:], tab_words[a].rearrange("p t i -> p (t i)").bitcast(I32))
-        w1_rows = w1.rearrange("(a p i) c -> a p i c", p=P, i=PACK)
-        w1_raw = []
-        for a in range(PASSES):
-            parts = 2 if a == PASSES - 1 else 1
-            width = H // parts
-            w1_raw.append([held([P, PACK, width], F32, f"w1_raw{a}_{u}") for u in range(parts)])
-            for u in range(parts):
-                nc.sync.dma_start(w1_raw[a][u][:], w1_rows[a][:, :, u * width : (u + 1) * width])
         rg_sb = held([P, PACK], F32, "rg_sb")
-        nc.sync.dma_start(p1[:], pos1)
-        nc.sync.dma_start(p2[:], pos2)
-        nc.sync.dma_start(rg_sb[:], rg.rearrange("(p t) -> p t", t=PACK))
-        nc.sync.dma_start(p3[:], pos3)
-        w2_raw = held([P, PACK, H], F32, "w2_raw")
-        nc.sync.dma_start(w2_raw[:], w2.rearrange("(p i) c -> p i c", i=PACK))
+        w4_raw = held([P, PASSES, 2 * H], U8, "w4_raw")
+        table = []
 
-        for q in range(4):
-            nc.gpsimd.dma_start(
-                table_scales[32 * q : 32 * q + 4 * PASSES, :].bitcast(I32),
-                tab_scales[:, 4 * q : 4 * q + 4, :].bitcast(I32),
-            )
-        for q in range(4):
-            nc.gpsimd.dma_start(
+        def load_words(a, t0, t1):
+            words = tab_words[a].rearrange("p t i -> p (t i)").bitcast(I32)
+            nc.sync.dma_start(table[a][:, t0:t1], words[:, t0:t1])
+
+        def load_table(a):
+            table.append(held([P, T], I32, f"region{a}"))
+            load_words(a, 0, T)
+
+        def load_w4_scales(q):
+            nc.sync.dma_start(
                 w4_scales_raw[32 * q : 32 * q + 4, :, :].bitcast(I32),
                 w4_scales[:, 4 * q : 4 * q + 4, :].rearrange("a r c -> r a c").bitcast(I32),
             )
 
-        nc.vector.tensor_copy(v_scales[0][:], table_scales[:].indirect(idx[:]))
-        for a in range(1, PASSES):
-            nc.gpsimd.dma_start(
-                v_scales[a][0:SHIFT_ROWS, :].bitcast(I32),
-                v_scales[0][4 * a : 4 * a + SHIFT_ROWS, :].bitcast(I32),
+        table_row0 = 32 - 4 * PASSES
+        nc.vector.memset(w4_scales_raw[:].rearrange("p a c -> p (a c)").bitcast(I32), 0)
+        for q in range(4):
+            nc.vector.memset(table_scales[32 * q : 32 * q + table_row0, :].bitcast(I32), 0)
+        table.append(held([P, T], I32, "region0"))
+        load_words(0, 0, T // 2)
+        nc.sync.dma_start(idx[:], offs)
+        for q in range(4):
+            nc.sync.dma_start(
+                table_scales[32 * q + table_row0 : 32 * (q + 1), :].bitcast(I32),
+                tab_scales[:, 4 * q : 4 * q + 4, :].bitcast(I32),
             )
+        load_words(0, T // 2, T)
+        for q in range(4):
+            load_w4_scales(q)
+        nc.sync.dma_start(w4_raw[:].bitcast(I32), w4_words.rearrange("a p c -> p a c").bitcast(I32))
+        load_table(1)
+        nc.sync.dma_start(p1[:], pos1)
+        nc.sync.dma_start(p2[:], pos2)
+        nc.sync.dma_start(p3[:], pos3)
+        nc.gpsimd.dma_start(gain_sb[:], gain.rearrange("(p t) -> p t", t=PACK))
+        nc.gpsimd.dma_start(rg_sb[:], rg.rearrange("(p t) -> p t", t=PACK))
+        for a in range(PASSES):
+            nc.gpsimd.memset(v_scales[a][96:P, :].bitcast(I32), 0)
 
-        w4_codes = held([P, PASSES, 2 * H], U8, "w4_codes")
-        w4_planes = held([P, PASSES, H], U8, "w4_planes")
-        nc.vector.tensor_copy(
-            w4_codes[:].bitcast(U16).rearrange("p a (t m) -> p a m t", t=PACK),
-            w4_raw[:].bitcast(U16).rearrange("p a (m t) -> p a m t", t=PACK),
-        )
+        picked_scales = held([P, S], U8, "picked_scales")
+        nc.vector.tensor_copy(picked_scales[:], table_scales[:].indirect(idx[:]))
+        for a in range(PASSES):
+            row0 = table_row0 + 4 * a
+            nc.sync.dma_start(
+                v_scales[a][0:SHIFT_ROWS, :].bitcast(I32),
+                picked_scales[row0 : row0 + SHIFT_ROWS, :].bitcast(I32),
+            )
+        load_table(2)
+
         nc.vector.tensor_copy(
             w4_planes[:].rearrange("p a (t m) -> p a m t", t=PACK),
             w4_scales_raw[:].rearrange("p a (m t) -> p a m t", t=PACK),
         )
-
-        gain_wide = [held([P, M], F32, f"gain_wide{t}") for t in range(PACK)]
-        for t in range(PACK):
-            nc.vector.tensor_copy(gain_wide[t][:], gain_sb[:, t : t + 1].to_broadcast([P, M]))
+        w4_codes = held([P, PASSES, 2 * H], U8, "w4_codes")
+        nc.vector.tensor_copy(
+            w4_codes[:].bitcast(U16).rearrange("p a (t m) -> p a m t", t=PACK),
+            w4_raw[:].bitcast(U16).rearrange("p a (m t) -> p a m t", t=PACK),
+        )
 
         v_codes = [held([P, S], U32, f"v_codes{a}") for a in range(PASSES)]
         for a in range(PASSES):
@@ -119,6 +122,17 @@ def tile_list_rifle_sway_evaluator_kernel(
                         v_codes[a][:, u * BANK : (u + 1) * BANK],
                         window.indirect(idx[:, u * BANK // 16 : (u + 1) * BANK // 16]),
                     )
+
+        w1_rows = w1.rearrange("(a p i) c -> a p i c", p=P, i=PACK)
+        w1_raw = []
+        for a, (name, parts) in enumerate([("region0", 1), ("region1", 1), ("region2", 2)]):
+            width = H // parts
+            raw = held([P, parts * PACK * width], F32, name)
+            w1_raw.append([])
+            for u in range(parts):
+                part = raw[:, u * PACK * width : (u + 1) * PACK * width].rearrange("p (i c) -> p i c", i=PACK)
+                nc.sync.dma_start(part, w1_rows[a][:, :, u * width : (u + 1) * width])
+                w1_raw[a].append(part)
 
         def bank(b):
             return psum.tile([P, BANK], F32, name=f"bank{b}")
@@ -148,8 +162,11 @@ def tile_list_rifle_sway_evaluator_kernel(
             for u in range(HALVES):
                 nc.scalar.activation(cos_part[t][:, cols(u)], drift[t][u][:], ACT.Sin, scale=0.5)
 
+        squares = []
+
         def drift_square(t):
-            nc.scalar.activation(cos_part[t][:], cos_part[t][:], ACT.Square, scale=math.sqrt(2.0))
+            squares.append(ring.tile([P, S], F32, name="square"))
+            nc.scalar.activation(squares[t][:], cos_part[t][:], ACT.Square, scale=math.sqrt(2.0))
 
         drift_out(0)
         drift_out(1)
@@ -160,7 +177,7 @@ def tile_list_rifle_sway_evaluator_kernel(
         def deal(dst, src, m0, m1):
             return (
                 dst[:].rearrange("p (t m i) -> p m t i", t=PACK, i=PACK)[:, m0:m1],
-                src[:].rearrange("p i (m t) -> p m t i", t=PACK),
+                src.rearrange("p i (m t) -> p m t i", t=PACK),
             )
 
         w1_codes = [held([P, H], U32, f"w1_codes{a}") for a in range(PASSES)]
@@ -180,6 +197,14 @@ def tile_list_rifle_sway_evaluator_kernel(
                         rounded[:, t * H : (t + 1) * H],
                     )
 
+        gain_wide = [held([P, M], F32, f"gain_wide{t}") for t in range(PACK)]
+        for t in range(PACK):
+            nc.gpsimd.tensor_scalar(
+                gain_wide[t][:], gain_sb[:, t : t + 1].to_broadcast([P, M]), 1.0, 0.0, ALU.mult, ALU.add
+            )
+
+        w2_raw = held([P, PACK, H], F32, "region0")
+        nc.sync.dma_start(w2_raw[:], w2.rearrange("(p i) c -> p i c", i=PACK))
         rg_neg = held([P, PACK], F32, "rg_neg")
         nc.vector.scalar_tensor_tensor(rg_neg[:], rg_sb[:], -1.0, gain_sb[:], ALU.mult, ALU.mult)
 
@@ -206,9 +231,9 @@ def tile_list_rifle_sway_evaluator_kernel(
         second = held([P, PACK, M], F32, "second")
 
         def make_h(t):
-            c = cos_part[t]
             if t > 0:
                 drift_square(t)
+            c = squares[t]
             sin_part = ring.tile([P, S], F32, name="sin_part")
             for u in range(HALVES):
                 nc.scalar.activation(sin_part[:, cols(u)], swing[t][u][:], ACT.Sin)
@@ -226,7 +251,7 @@ def tile_list_rifle_sway_evaluator_kernel(
             nc.vector.tensor_tensor(second[:, t, :], h[t][:].indirect(p2[:]), gain_wide[t][:], ALU.mult)
 
         w2_rounded = ring.tile([P, PACK * H], BF16, name="rounded", align_bytes=64)
-        nc.scalar.copy(*deal(w2_rounded, w2_raw, 0, P))
+        nc.scalar.copy(*deal(w2_rounded, w2_raw[:], 0, P))
         w2_codes = held([P, H], U32, "w2_codes")
         w2_plane = held([P, H], U8, "w2_plane")
         nc.vector.quantize_mx(w2_codes[:].bitcast(FP8X4), w2_plane[:], w2_rounded[:])
@@ -239,52 +264,68 @@ def tile_list_rifle_sway_evaluator_kernel(
 
         make_cos_hs(0)
 
-        half = M // 2
-        x_rounded = [held([P, PACK * half], BF16, f"x_rounded{u}") for u in range(2)]
-        x_codes = [held([P, half], U32, f"x_codes{u}") for u in range(2)]
-        x_plane = [held([P, half], U8, f"x_plane{u}") for u in range(2)]
-        for u in range(2):
-            span = slice(u * half, (u + 1) * half)
+        pieces = [slice(0, 256), slice(256, 384), slice(384, 512)]
+        widths = [s.stop - s.start for s in pieces]
+        x_rounded = [held([P, PACK * w], BF16, f"x_rounded{u}") for u, w in enumerate(widths)]
+        x_codes = [held([P, w], U32, f"x_codes{u}") for u, w in enumerate(widths)]
+        x_plane = [held([P, w], U8, f"x_plane{u}") for u, w in enumerate(widths)]
+
+        def pair_max(u):
             nc.vector.tensor_tensor(
                 x_rounded[u][:].rearrange("p (c i t) -> p c t i", i=4, t=PACK),
-                first[:, :, span].rearrange("p t (c i) -> p c t i", i=4),
-                second[:, :, span].rearrange("p t (c i) -> p c t i", i=4),
+                first[:, :, pieces[u]].rearrange("p t (c i) -> p c t i", i=4),
+                second[:, :, pieces[u]].rearrange("p t (c i) -> p c t i", i=4),
                 ALU.max,
             )
-        for u in range(2):
+
+        pair_max(0)
+        for u in range(len(pieces)):
+            if u + 1 < len(pieces):
+                pair_max(u + 1)
             nc.vector.quantize_mx(x_codes[u][:].bitcast(FP8X4), x_plane[u][:], x_rounded[u][:])
 
         y = [held([P, M + SPARE], F32, f"y{t}") for t in range(PACK)]
         for t in range(PACK):
             nc.gpsimd.memset(y[t][:, M:], 0.0)
+
+        def second_product(t, u, acc):
+            nc.tensor.matmul_mx(
+                acc,
+                lhsT=w2_codes[:, rows(t)].bitcast(FP8X4),
+                lhsT_scale=w2_plane[:, rows(t)],
+                rhs=x_codes[u][:].bitcast(FP8X4),
+                rhs_scale=x_plane[u][:],
+                start=True,
+                stop=True,
+            )
+
         for t in range(PACK):
-            for u in range(2):
-                acc = psum.tile([P, half], F32, name=f"bank{2 * t + u}")
-                nc.tensor.matmul_mx(
-                    acc[:],
-                    lhsT=w2_codes[:, rows(t)].bitcast(FP8X4),
-                    lhsT_scale=w2_plane[:, rows(t)],
-                    rhs=x_codes[u][:].bitcast(FP8X4),
-                    rhs_scale=x_plane[u][:],
-                    start=True,
-                    stop=True,
-                )
-                nc.scalar.copy(y[t][:, u * half : (u + 1) * half], acc[:])
+            if t == 0:
+                for u in range(len(pieces)):
+                    acc = psum.tile([P, widths[u]], F32, name=f"bank{u}")
+                    second_product(t, u, acc[:])
+                    nc.scalar.copy(y[t][:, pieces[u]], acc[:])
+            else:
+                acc = bank(len(pieces) + t)
+                for u in range(len(pieces)):
+                    second_product(t, u, acc[:, pieces[u]])
+                nc.scalar.copy(y[t][:, :M], acc[:])
             if t + 1 < PACK:
                 make_cos_hs(t + 1)
 
         out_rows = out.rearrange("(p t) j -> p t j", t=PACK)
         for t in range(PACK):
-            scores = [held([P, BANK], F32, f"score{t}_{u}") for u in range(HALVES)]
-            for u in range(HALVES):
+            spans = [cols(0), cols(1)] if t + 1 < PACK else [cols(0), slice(512, 768), slice(768, S)]
+            scores = [held([P, s.stop - s.start], F32, f"score{t}_{u}") for u, s in enumerate(spans)]
+            for u, s in enumerate(spans):
                 nc.vector.tensor_tensor(
                     scores[u][:],
-                    y[t][:].indirect(p3[:, u * BANK // 16 : (u + 1) * BANK // 16]),
-                    cos_hs[t][:, cols(u)],
+                    y[t][:].indirect(p3[:, s.start // 16 : s.stop // 16]),
+                    cos_hs[t][:, s],
                     ALU.mult,
                 )
-            for u in range(HALVES):
+            for u, s in enumerate(spans):
                 nc.vector.scalar_tensor_tensor(
-                    scores[u][:], h[t][:, cols(u)], rg_neg[:, t : t + 1], scores[u][:], ALU.mult, ALU.add
+                    scores[u][:], h[t][:, s], rg_neg[:, t : t + 1], scores[u][:], ALU.mult, ALU.add
                 )
-                nc.sync.dma_start(out_rows[:, t, cols(u)], scores[u][:])
+                nc.sync.dma_start(out_rows[:, t, s], scores[u][:])

import math
from contextlib import ExitStack

import concourse.mybir as mybir

K, T, S, M, H = 1536, 4096, 1024, 512, 512
FLOPS = 2 * K * H * S * 2 + 2 * H * H * M

F32 = mybir.dt.float32
BF16 = mybir.dt.bfloat16
I32 = mybir.dt.int32
U32 = mybir.dt.uint32
U16 = mybir.dt.uint16
U8 = mybir.dt.uint8
FP8X4 = mybir.dt.float8_e4m3fn_x4
FP4X4 = mybir.dt.float4_e2m1fn_x4
ACT = mybir.ActivationFunctionType
ALU = mybir.AluOpType

P = 128
PACK = 4
PASSES = K // (P * PACK)
BANK = 512
HALVES = S // BANK
SPARE = 16
SHIFT_ROWS = 100


def tile_list_rifle_sway_evaluator_kernel(
    tc, tab_words, tab_scales, offs, pos1, pos2, pos3, w1, w4_words, w4_scales, gain, w2, rg, out
):
    nc = tc.nc
    with ExitStack() as ctx:
        keep = ctx.enter_context(tc.tile_pool(name="keep", bufs=1))
        ring = ctx.enter_context(tc.tile_pool(name="ring", bufs=2))
        psum = ctx.enter_context(tc.psum_pool(name="psum", bufs=1))

        def held(shape, dtype, name):
            return keep.tile(shape, dtype, name=name, align_bytes=64)

        idx = keep.tile([P, S // 16], U16, name="idx")
        p1 = keep.tile([P, M // 16], U16, name="p1")
        p2 = keep.tile([P, M // 16], U16, name="p2")
        p3 = keep.tile([P, S // 16], U16, name="p3")

        table_scales = held([P, T], U8, "region2")
        w4_scales_raw = held([P, PASSES, H], U8, "w4_scales_raw")
        v_scales = [held([P, S], U8, f"v_scales{a}") for a in range(PASSES)]
        w4_planes = held([P, PASSES, H], U8, "w4_planes")
        gain_sb = held([P, PACK], F32, "gain_sb")
        rg_sb = held([P, PACK], F32, "rg_sb")
        w4_raw = held([P, PASSES, 2 * H], U8, "w4_raw")
        table = []

        def load_words(a, t0, t1):
            words = tab_words[a].rearrange("p t i -> p (t i)").bitcast(I32)
            nc.sync.dma_start(table[a][:, t0:t1], words[:, t0:t1])

        def load_table(a):
            table.append(held([P, T], I32, f"region{a}"))
            load_words(a, 0, T)

        def load_w4_scales(q):
            nc.sync.dma_start(
                w4_scales_raw[32 * q : 32 * q + 4, :, :].bitcast(I32),
                w4_scales[:, 4 * q : 4 * q + 4, :].rearrange("a r c -> r a c").bitcast(I32),
            )

        table_row0 = 32 - 4 * PASSES
        nc.vector.memset(w4_scales_raw[:].rearrange("p a c -> p (a c)").bitcast(I32), 0)
        for q in range(4):
            nc.vector.memset(table_scales[32 * q : 32 * q + table_row0, :].bitcast(I32), 0)
        table.append(held([P, T], I32, "region0"))
        load_words(0, 0, T // 2)
        nc.sync.dma_start(idx[:], offs)
        for q in range(4):
            nc.sync.dma_start(
                table_scales[32 * q + table_row0 : 32 * (q + 1), :].bitcast(I32),
                tab_scales[:, 4 * q : 4 * q + 4, :].bitcast(I32),
            )
        load_words(0, T // 2, T)
        for q in range(4):
            load_w4_scales(q)
        nc.sync.dma_start(w4_raw[:].bitcast(I32), w4_words.rearrange("a p c -> p a c").bitcast(I32))
        load_table(1)
        nc.sync.dma_start(p1[:], pos1)
        nc.sync.dma_start(p2[:], pos2)
        nc.sync.dma_start(p3[:], pos3)
        nc.gpsimd.dma_start(gain_sb[:], gain.rearrange("(p t) -> p t", t=PACK))
        nc.gpsimd.dma_start(rg_sb[:], rg.rearrange("(p t) -> p t", t=PACK))
        for a in range(PASSES):
            nc.gpsimd.memset(v_scales[a][96:P, :].bitcast(I32), 0)

        picked_scales = held([P, S], U8, "picked_scales")
        nc.vector.tensor_copy(picked_scales[:], table_scales[:].indirect(idx[:]))
        for a in range(PASSES):
            row0 = table_row0 + 4 * a
            nc.sync.dma_start(
                v_scales[a][0:SHIFT_ROWS, :].bitcast(I32),
                picked_scales[row0 : row0 + SHIFT_ROWS, :].bitcast(I32),
            )
        load_table(2)

        nc.vector.tensor_copy(
            w4_planes[:].rearrange("p a (t m) -> p a m t", t=PACK),
            w4_scales_raw[:].rearrange("p a (m t) -> p a m t", t=PACK),
        )
        w4_codes = held([P, PASSES, 2 * H], U8, "w4_codes")
        nc.vector.tensor_copy(
            w4_codes[:].bitcast(U16).rearrange("p a (t m) -> p a m t", t=PACK),
            w4_raw[:].bitcast(U16).rearrange("p a (m t) -> p a m t", t=PACK),
        )

        v_codes = [held([P, S], U32, f"v_codes{a}") for a in range(PASSES)]
        for a in range(PASSES):
            window = table[a][:].bitcast(U32)
            if a < PASSES - 1:
                nc.vector.tensor_copy(v_codes[a][:], window.indirect(idx[:]))
            else:
                for u in range(HALVES):
                    nc.vector.tensor_copy(
                        v_codes[a][:, u * BANK : (u + 1) * BANK],
                        window.indirect(idx[:, u * BANK // 16 : (u + 1) * BANK // 16]),
                    )

        w1_rows = w1.rearrange("(a p i) c -> a p i c", p=P, i=PACK)
        w1_raw = []
        for a, (name, parts) in enumerate([("region0", 1), ("region1", 1), ("region2", 2)]):
            width = H // parts
            raw = held([P, parts * PACK * width], F32, name)
            w1_raw.append([])
            for u in range(parts):
                part = raw[:, u * PACK * width : (u + 1) * PACK * width].rearrange("p (i c) -> p i c", i=PACK)
                nc.sync.dma_start(part, w1_rows[a][:, :, u * width : (u + 1) * width])
                w1_raw[a].append(part)

        def bank(b):
            return psum.tile([P, BANK], F32, name=f"bank{b}")

        def cols(u):
            return slice(u * BANK, (u + 1) * BANK)

        def rows(t):
            return slice(t * P, (t + 1) * P)

        drift = [[bank(HALVES * t + u) for u in range(HALVES)] for t in range(PACK)]
        for a in range(PASSES):
            for u in range(HALVES):
                for t in range(PACK):
                    nc.tensor.matmul_mx(
                        drift[t][u][:],
                        lhsT=w4_codes[:, a, 2 * t * P : 2 * (t + 1) * P].bitcast(FP4X4),
                        lhsT_scale=w4_planes[:, a, rows(t)],
                        rhs=v_codes[a][:, cols(u)].bitcast(FP8X4),
                        rhs_scale=v_scales[a][:, cols(u)],
                        start=(a == 0),
                        stop=(a == PASSES - 1),
                    )
        cos_part = [held([P, S], F32, f"cos_part{t}") for t in range(PACK)]

        def drift_out(t):
            for u in range(HALVES):
                nc.scalar.activation(cos_part[t][:, cols(u)], drift[t][u][:], ACT.Sin, scale=0.5)

        squares = []

        def drift_square(t):
            squares.append(ring.tile([P, S], F32, name="square"))
            nc.scalar.activation(squares[t][:], cos_part[t][:], ACT.Square, scale=math.sqrt(2.0))

        drift_out(0)
        drift_out(1)
        drift_square(0)
        drift_out(2)
        drift_out(3)

        def deal(dst, src, m0, m1):
            return (
                dst[:].rearrange("p (t m i) -> p m t i", t=PACK, i=PACK)[:, m0:m1],
                src.rearrange("p i (m t) -> p m t i", t=PACK),
            )

        w1_codes = [held([P, H], U32, f"w1_codes{a}") for a in range(PASSES)]
        w1_planes = [held([P, H], U8, f"w1_planes{a}") for a in range(PASSES)]
        for a in range(PASSES):
            rounded = ring.tile([P, PACK * H], BF16, name="rounded", align_bytes=64)
            parts = len(w1_raw[a])
            for u in range(parts):
                nc.vector.tensor_copy(*deal(rounded, w1_raw[a][u], u * P // parts, (u + 1) * P // parts))
            if a < PASSES - 1:
                nc.vector.quantize_mx(w1_codes[a][:].bitcast(FP8X4), w1_planes[a][:], rounded[:])
            else:
                for t in range(PACK):
                    nc.vector.quantize_mx(
                        w1_codes[a][:, rows(t)].bitcast(FP8X4),
                        w1_planes[a][:, rows(t)],
                        rounded[:, t * H : (t + 1) * H],
                    )

        gain_wide = [held([P, M], F32, f"gain_wide{t}") for t in range(PACK)]
        for t in range(PACK):
            nc.gpsimd.tensor_scalar(
                gain_wide[t][:], gain_sb[:, t : t + 1].to_broadcast([P, M]), 1.0, 0.0, ALU.mult, ALU.add
            )

        w2_raw = held([P, PACK, H], F32, "region0")
        nc.sync.dma_start(w2_raw[:], w2.rearrange("(p i) c -> p i c", i=PACK))
        rg_neg = held([P, PACK], F32, "rg_neg")
        nc.vector.scalar_tensor_tensor(rg_neg[:], rg_sb[:], -1.0, gain_sb[:], ALU.mult, ALU.mult)

        swing = [[bank(HALVES * t + u) for u in range(HALVES)] for t in range(PACK)]

        def swing_pass(a, t):
            for u in range(HALVES):
                nc.tensor.matmul_mx(
                    swing[t][u][:],
                    lhsT=w1_codes[a][:, rows(t)].bitcast(FP8X4),
                    lhsT_scale=w1_planes[a][:, rows(t)],
                    rhs=v_codes[a][:, cols(u)].bitcast(FP8X4),
                    rhs_scale=v_scales[a][:, cols(u)],
                    start=(a == 0),
                    stop=(a == PASSES - 1),
                )

        for t in range(PACK):
            for a in range(PASSES):
                swing_pass(a, t)

        h = [held([P, S], F32, f"h{t}") for t in range(PACK)]
        first = held([P, PACK, M], F32, "first")
        second = held([P, PACK, M], F32, "second")

        def make_h(t):
            if t > 0:
                drift_square(t)
            c = squares[t]
            sin_part = ring.tile([P, S], F32, name="sin_part")
            for u in range(HALVES):
                nc.scalar.activation(sin_part[:, cols(u)], swing[t][u][:], ACT.Sin)
            spans = [cols(u) for u in range(HALVES)] if t == 0 else [slice(0, S)]
            for span in spans:
                nc.vector.scalar_tensor_tensor(
                    h[t][:, span], sin_part[:, span], 1.0, c[:, span], ALU.add, ALU.subtract
                )

        make_h(0)
        for t in range(PACK):
            nc.vector.tensor_tensor(first[:, t, :], h[t][:].indirect(p1[:]), gain_wide[t][:], ALU.mult)
            if t + 1 < PACK:
                make_h(t + 1)
            nc.vector.tensor_tensor(second[:, t, :], h[t][:].indirect(p2[:]), gain_wide[t][:], ALU.mult)

        w2_rounded = ring.tile([P, PACK * H], BF16, name="rounded", align_bytes=64)
        nc.scalar.copy(*deal(w2_rounded, w2_raw[:], 0, P))
        w2_codes = held([P, H], U32, "w2_codes")
        w2_plane = held([P, H], U8, "w2_plane")
        nc.vector.quantize_mx(w2_codes[:].bitcast(FP8X4), w2_plane[:], w2_rounded[:])

        cos_hs = [keep.tile([P, S], F32, name=f"cos_part{t}", align_bytes=64) for t in range(PACK)]

        def make_cos_hs(t):
            nc.scalar.activation(cos_hs[t][:], h[t][:], ACT.Abs, scale=rg_neg[:, t : t + 1])
            nc.scalar.activation(cos_hs[t][:], cos_hs[t][:], ACT.Sin, scale=-1.0, bias=math.pi / 2)

        make_cos_hs(0)

        pieces = [slice(0, 256), slice(256, 384), slice(384, 512)]
        widths = [s.stop - s.start for s in pieces]
        x_rounded = [held([P, PACK * w], BF16, f"x_rounded{u}") for u, w in enumerate(widths)]
        x_codes = [held([P, w], U32, f"x_codes{u}") for u, w in enumerate(widths)]
        x_plane = [held([P, w], U8, f"x_plane{u}") for u, w in enumerate(widths)]

        def pair_max(u):
            nc.vector.tensor_tensor(
                x_rounded[u][:].rearrange("p (c i t) -> p c t i", i=4, t=PACK),
                first[:, :, pieces[u]].rearrange("p t (c i) -> p c t i", i=4),
                second[:, :, pieces[u]].rearrange("p t (c i) -> p c t i", i=4),
                ALU.max,
            )

        pair_max(0)
        for u in range(len(pieces)):
            if u + 1 < len(pieces):
                pair_max(u + 1)
            nc.vector.quantize_mx(x_codes[u][:].bitcast(FP8X4), x_plane[u][:], x_rounded[u][:])

        y = [held([P, M + SPARE], F32, f"y{t}") for t in range(PACK)]
        for t in range(PACK):
            nc.gpsimd.memset(y[t][:, M:], 0.0)

        def second_product(t, u, acc):
            nc.tensor.matmul_mx(
                acc,
                lhsT=w2_codes[:, rows(t)].bitcast(FP8X4),
                lhsT_scale=w2_plane[:, rows(t)],
                rhs=x_codes[u][:].bitcast(FP8X4),
                rhs_scale=x_plane[u][:],
                start=True,
                stop=True,
            )

        for t in range(PACK):
            if t == 0:
                for u in range(len(pieces)):
                    acc = psum.tile([P, widths[u]], F32, name=f"bank{u}")
                    second_product(t, u, acc[:])
                    nc.scalar.copy(y[t][:, pieces[u]], acc[:])
            else:
                acc = bank(len(pieces) + t)
                for u in range(len(pieces)):
                    second_product(t, u, acc[:, pieces[u]])
                nc.scalar.copy(y[t][:, :M], acc[:])
            if t + 1 < PACK:
                make_cos_hs(t + 1)

        out_rows = out.rearrange("(p t) j -> p t j", t=PACK)
        for t in range(PACK):
            spans = [cols(0), cols(1)] if t + 1 < PACK else [cols(0), slice(512, 768), slice(768, S)]
            scores = [held([P, s.stop - s.start], F32, f"score{t}_{u}") for u, s in enumerate(spans)]
            for u, s in enumerate(spans):
                nc.vector.tensor_tensor(
                    scores[u][:],
                    y[t][:].indirect(p3[:, s.start // 16 : s.stop // 16]),
                    cos_hs[t][:, s],
                    ALU.mult,
                )
            for u, s in enumerate(spans):
                nc.vector.scalar_tensor_tensor(
                    scores[u][:], h[t][:, s], rg_neg[:, t : t + 1], scores[u][:], ALU.mult, ALU.add
                )
                nc.sync.dma_start(out_rows[:, t, s], scores[u][:])
